import numpy as np
import ml_dtypes


def mxq(x, axis, fmt="e4m3"):
    dtype, down = {"e4m3": (ml_dtypes.float8_e4m3fn, 7), "e5m2": (ml_dtypes.float8_e5m2, 14)}[fmt]
    v = np.moveaxis(np.asarray(x, np.float32).astype(ml_dtypes.bfloat16).astype(np.float64), axis, -1)
    blocks = v.reshape(v.shape[:-1] + (-1, 32))
    amax = np.abs(blocks).max(-1, keepdims=True)
    byte = np.maximum(np.where(amax > 0, np.frexp(amax)[1] - 1 + 127, 0) - down, 1)
    scale = np.exp2(byte - 127.0)
    codes = (blocks / scale).astype(np.float32).astype(dtype).astype(np.float64)
    return np.moveaxis((codes * scale).reshape(v.shape), -1, axis)


WIDE = False


def mx_kscale(k):
    if not WIDE:
        return np.ones(k)
    levels = np.array([10, -10, 5, -5, 0])
    if k % 512:
        return np.exp2(np.random.permutation(np.resize(levels, k // 32))).repeat(32)
    a = np.empty((k // 512, 16))
    for p in range(k // 512):
        a[p, :8] = np.random.permutation(np.resize(levels, 8))
        for g in range(8):
            far = levels[np.abs(levels - a[p, g]) >= 10]
            a[p, g + 8] = far[np.random.randint(len(far))]
    return np.exp2(a.ravel()).repeat(32)


def f64(x):
    return np.asarray(x).astype(np.float64)


def striped(idx):
    return np.tile(idx.reshape(-1, 16).T, (8, 1)).astype(np.uint16)


def unstriped(offs):
    return offs[:16].T.reshape(-1).astype(np.int64)


def striped8(idx):
    return np.concatenate([x.reshape(-1, 16).T for x in idx]).astype(np.uint16)


def runs(offs, k):
    lists = np.stack([offs[16 * r : 16 * r + 16].T.reshape(-1) for r in range(8)]).astype(np.int64)
    return lists[np.arange(k) % 512 // 64]


def pack_weight(w):
    k, n = w.shape
    w = f64(np.asarray(w, np.float32).astype(ml_dtypes.bfloat16)).reshape(k // 32, 32, n)
    amax = np.abs(w).max(1)
    byte = np.clip(np.where(amax > 0, np.frexp(amax)[1] - 1 + 127 - 7, 1), 1, 254)
    scaled = (w * np.exp2(127.0 - byte)[:, None, :]).reshape(k, n).astype(np.float32)
    words = np.ascontiguousarray(scaled.reshape(k // 512, 128, 4, n).transpose(0, 1, 3, 2)).astype(ml_dtypes.float8_e4m3fn).view(np.uint8)
    return words, np.ascontiguousarray(byte.astype(np.uint8).reshape(k // 512, 16, n))


def unpack_weight(words, scales):
    g, p, n, _ = words.shape
    vals = np.ascontiguousarray(words).view(ml_dtypes.float8_e4m3fn).astype(np.float64) * np.repeat(np.exp2(scales.astype(np.float64) - 127.0), 8, axis=1)[..., None]
    return vals.transpose(0, 1, 3, 2).reshape(g * 512, n)


E2M1 = np.array([0.0, 0.5, 1.0, 1.5, 2.0, 3.0, 4.0, 6.0, -0.0, -0.5, -1.0, -1.5, -2.0, -3.0, -4.0, -6.0])


def pack_fp4(w):
    k, n = w.shape
    w = f64(np.asarray(w, np.float32).astype(ml_dtypes.bfloat16)).reshape(k // 32, 32, n)
    amax = np.abs(w).max(1)
    mant, ex = np.frexp(amax / 6.0)
    byte = np.clip(np.where(amax > 0, np.where(mant > 0.5, ex, ex - 1) + 127, 1), 1, 254)
    scaled = (w * np.exp2(127.0 - byte)[:, None, :]).reshape(k, n).astype(np.float32)
    c = np.ascontiguousarray(scaled.reshape(k // 512, 128, 4, n).transpose(0, 1, 3, 2)).astype(ml_dtypes.float4_e2m1fn).view(np.uint8) & 0xF
    words = (c[..., 0::2] | (c[..., 1::2] << 4)).reshape(k // 512, 128, 2 * n)
    return np.ascontiguousarray(words), np.ascontiguousarray(byte.astype(np.uint8).reshape(k // 512, 16, n))


def unpack_fp4(words, scales):
    g, _, n = scales.shape
    words = np.ascontiguousarray(words).reshape(g, 128, n, 2)
    nib = np.empty((g, 128, n, 4), np.uint8)
    nib[..., 0::2] = words & 0xF
    nib[..., 1::2] = words >> 4
    vals = E2M1[nib] * np.repeat(np.exp2(scales.astype(np.float64) - 127.0), 8, axis=1)[..., None]
    return vals.transpose(0, 1, 3, 2).reshape(g * 512, n)


def planes(y):
    n, m = y.shape
    v = y.astype(np.float32).astype(ml_dtypes.bfloat16).astype(np.float64).reshape(n // 32, 32, m)
    top = np.abs(v).max(1)
    byte = np.clip(np.where(top > 0, np.frexp(top)[1] - 1 + 127 - 7, 1), 1, 254)
    codes = (v * np.exp2(127.0 - byte)[:, None, :]).reshape(n, m).astype(np.float32).astype(ml_dtypes.float8_e4m3fn).view(np.uint8)
    words = codes.reshape(n // 512, 128, 4, m).transpose(0, 1, 3, 2)
    return np.ascontiguousarray(words), np.ascontiguousarray(byte.astype(np.uint8).reshape(n // 512, 16, m))


K, T, S, N, H, W, C = 512, 2048, 512, 512, 512, 384, 512


def setup_inputs():
    n = np.random.standard_normal
    s = mx_kscale(K)[:, None]
    u = mx_kscale(S)
    packed_xT = pack_weight(n((K, T)) * s)
    packed_w1 = pack_fp4(n((K, H)) / np.sqrt(K) / s)
    packed_w2 = pack_fp4(n((K, H)) / np.sqrt(K) / s)
    packed_w3 = pack_fp4(n((H, N)) / np.sqrt(H) / u[:, None])
    return {
        "x_words": packed_xT[0],
        "x_scales": packed_xT[1],
        "w1_words": packed_w1[0],
        "w1_scales": packed_w1[1],
        "w2_words": packed_w2[0],
        "w2_scales": packed_w2[1],
        "gn": (np.random.uniform(0.5, 1.5, (H, 1)) * u[:, None]).astype(np.float32),
        "w3_words": packed_w3[0],
        "w3_scales": packed_w3[1],
        "gs": (np.random.uniform(0.5, 1.5, (K, 1)) / s).astype(np.float32),
        "offs": striped(np.random.permutation(T)[:S]),
        "two": striped(np.random.permutation(T)[:S]),
        "n1": striped8(np.stack([np.random.permutation(S) for _ in range(8)])),
        "n2": striped(np.random.permutation(S)[:W]),
        "n3": striped(np.random.permutation(S)[:W]),
        "cand": striped(np.random.permutation(T)[:C]),
        "n4": striped(np.random.permutation(S)),
        "n5": striped(np.random.permutation(S)),
    }


def reference(x_words, x_scales, w1_words, w1_scales, w2_words, w2_scales, gn, w3_words, w3_scales, gs, offs, two, n1, n2, n3, cand, n4, n5):
    xq = unpack_weight(x_words, x_scales)[:, unstriped(offs)]
    y = unpack_fp4(w1_words, w1_scales).T @ xq
    z = f64(gn) * (y - (y[np.arange(H)[:, None], runs(n1, H)]))
    a = unpack_fp4(w3_words, w3_scales).T @ mxq(z, 0, "e4m3")
    x_cand = unpack_weight(x_words, x_scales)[:, unstriped(cand)]
    x_two = unpack_weight(x_words, x_scales)[:, unstriped(two)]
    d = unpack_fp4(w2_words, w2_scales).T @ x_two
    pa = d[:, unstriped(n3)]
    old = d[:, unstriped(n2)]
    ra = np.maximum(pa, 0.5 * old)
    ds = d.copy()
    ds[:, unstriped(n2)] = ra
    z2 = f64(gs) * ds
    b = 0.0625 * ((x_cand.T @ mxq(z2, 0, "e4m3")))
    out_0 = 0.75 * (a * b[:, unstriped(n5)] - (a[:, unstriped(n4)] * b))
    return (out_0,) + planes(out_0)

@@ -1,0 +1,239 @@
+from contextlib import ExitStack
+
+import concourse.mybir as mybir
+
+K, T, S, W = 512, 2048, 512, 384
+P = 128
+PACK = 4
+HALF = S // 2
+FLOPS = 4 * 2 * 512 * 512 * 512
+
+F32 = mybir.dt.float32
+BF16 = mybir.dt.bfloat16
+I32 = mybir.dt.int32
+U32 = mybir.dt.uint32
+U16 = mybir.dt.uint16
+U8 = mybir.dt.uint8
+FP8X4 = mybir.dt.float8_e4m3fn_x4
+FP4X4 = mybir.dt.float4_e2m1fn_x4
+ALU = mybir.AluOpType
+COPY = mybir.ActivationFunctionType.Copy
+
+
+def tile_picked_tfcdcrossbdifkmax_none_po_kernel(
+    tc, x_words, x_scales, w1_words, w1_scales, w2_words, w2_scales, gn, w3_words, w3_scales, gs,
+    offs, two, n1, n2, n3, cand, n4, n5, out_0, out_1, out_2,
+):
+    nc = tc.nc
+    with ExitStack() as ctx:
+        sb = ctx.enter_context(tc.tile_pool(name="sb", bufs=1))
+        psum = ctx.enter_context(tc.psum_pool(name="psum", bufs=1))
+
+        def new(shape, dtype, name):
+            return sb.tile(shape, dtype, name=name, align_bytes=64)
+
+        def load_list(src, name):
+            lst = new(list(src.shape), U16, name)
+            nc.sync.dma_start(lst[:], src)
+            return lst
+
+        def zeroed_plane(width, name, engine):
+            plane = new([P, width], U8, name)
+            engine.memset(plane[:].bitcast(I32), 0)
+            return plane
+
+        def load_scales(plane, src):
+            for q in range(4):
+                nc.sync.dma_start(plane[32 * q : 32 * q + 4, :].bitcast(I32), src[0, 4 * q : 4 * q + 4, :].bitcast(I32))
+
+        def load_fp4_words(src, name):
+            raw = new([P, 2 * S], U8, name)
+            nc.sync.dma_start(raw[:].bitcast(I32), src[0].bitcast(I32))
+            return raw
+
+        def load_gain(src, name):
+            gain = new([P, PACK], F32, name)
+            nc.sync.dma_start(gain[:], src.rearrange("(p t) o -> p (t o)", t=PACK))
+            return gain
+
+        def deal_fp4_words(raw, name):
+            dealt = new([P, 2 * S], U8, name)
+            nc.vector.tensor_copy(
+                dealt[:].rearrange("p (t m b) -> p t m b", t=PACK, b=2), raw[:].rearrange("p (m t b) -> p t m b", t=PACK, b=2)
+            )
+            return dealt
+
+        def deal_columns(raw, dtype, view, name):
+            dealt = new([P, S], dtype, name)
+            nc.vector.tensor_copy(
+                dealt[:].bitcast(view).rearrange("p (t m) -> p t m", t=PACK), raw[:].bitcast(view).rearrange("p (m t) -> p t m", t=PACK)
+            )
+            return dealt
+
+        def gather_packed(table, dtype, lst, name):
+            picked = new([P, S], dtype, name)
+            nc.vector.tensor_copy(picked[:], table[:].indirect(lst[:]))
+            return picked
+
+        def product(bank, lhs_words, lhs_scales, t, rhs_words, rhs_scales):
+            per = lhs_words.shape[1] // PACK
+            fmt = FP4X4 if per == 2 * P else FP8X4
+            acc = psum.tile([P, S], F32, name=bank)
+            nc.tensor.matmul_mx(
+                out=acc[:],
+                lhsT=lhs_words[:, per * t : per * (t + 1)].bitcast(fmt),
+                lhsT_scale=lhs_scales[:, P * t : P * (t + 1)],
+                rhs=rhs_words[:].bitcast(FP8X4),
+                rhs_scale=rhs_scales[:],
+                start=True,
+                stop=True,
+            )
+            return acc
+
+        def interleave(rows, width, name):
+            woven = new([P, width * PACK], BF16, name)
+            nc.vector.tensor_copy(
+                woven[:].rearrange("p (c i t) -> p c t i", i=4, t=PACK), rows[:].rearrange("p t (c i) -> p c t i", i=4)
+            )
+            return woven
+
+        def half_of(lst, h):
+            return lst[:, h * HALF // 16 : (h + 1) * HALF // 16]
+
+        xs = zeroed_plane(T, "xs", nc.gpsimd)
+        w2s_raw = zeroed_plane(S, "w2s_raw", nc.vector)
+        w1s_raw = zeroed_plane(S, "w1s_raw", nc.vector)
+        w3s_raw = zeroed_plane(S, "w3s_raw", nc.vector)
+        load_scales(xs, x_scales)
+        two_l = load_list(two, "two_l")
+        w2w_raw = load_fp4_words(w2_words, "w2w_raw")
+        w1w_raw = load_fp4_words(w1_words, "w1w_raw")
+        xw = new([P, T], U32, "xw")
+        nc.sync.dma_start(xw[:].bitcast(I32), x_words[0].rearrange("p n t -> p (n t)").bitcast(I32))
+        load_scales(w2s_raw, w2_scales)
+        offs_l = load_list(offs, "offs_l")
+        n3_l = load_list(n3, "n3_l")
+        n2_l = load_list(n2, "n2_l")
+        load_scales(w1s_raw, w1_scales)
+        gn_t = load_gain(gn, "gn_t")
+        n1_l = load_list(n1, "n1_l")
+        cand_l = load_list(cand, "cand_l")
+        w3w_raw = load_fp4_words(w3_words, "w3w_raw")
+        load_scales(w3s_raw, w3_scales)
+        gs_t = load_gain(gs, "gs_t")
+        n4_l = load_list(n4, "n4_l")
+        n5_l = load_list(n5, "n5_l")
+
+        two_s = gather_packed(xs, U8, two_l, "two_s")
+        w2w = deal_fp4_words(w2w_raw, "w2w")
+        w1w = deal_fp4_words(w1w_raw, "w1w")
+        two_w = gather_packed(xw, U32, two_l, "two_w")
+        w2s = deal_columns(w2s_raw, U8, U8, "w2s")
+        d_acc = [product("bank%d" % t, w2w, w2s, t, two_w, two_s) for t in range(PACK)]
+        offs_s = gather_packed(xs, U8, offs_l, "offs_s")
+        offs_w = gather_packed(xw, U32, offs_l, "offs_w")
+        w1s = deal_columns(w1s_raw, U8, U8, "w1s")
+        y_acc = [product("bank%d" % (PACK + t), w1w, w1s, t, offs_w, offs_s) for t in range(PACK)]
+
+        ds = [new([P, S], F32, "ds%d" % t) for t in range(PACK)]
+        pa = [new([P, W], F32, "pa%d" % t) for t in range(PACK)]
+        old = [new([P, W], F32, "old%d" % t) for t in range(PACK)]
+
+        def fetch_d(t):
+            nc.scalar.activation(ds[t][:], d_acc[t][:], COPY)
+            nc.scalar.activation(pa[t][:], ds[t][:].indirect(n3_l[:]), COPY)
+            nc.scalar.activation(old[t][:], ds[t][:].indirect(n2_l[:]), COPY)
+
+        def put_ra(t):
+            ra = new([P, W], F32, "ra")
+            nc.vector.scalar_tensor_tensor(ra[:], old[t][:], 0.5, pa[t][:], ALU.mult, ALU.max)
+            nc.vector.tensor_copy(ds[t][:].indirect(n2_l[:]), ra[:])
+
+        yg = [new([P, S], F32, "yg%d" % t) for t in range(PACK)]
+        yn = [new([P, S], F32, "yn%d" % t) for t in range(PACK)]
+        z_rows = new([P, PACK, S], BF16, "z_rows")
+
+        def fetch_y(t):
+            nc.scalar.activation(yg[t][:], y_acc[t][:], COPY, scale=gn_t[:, t : t + 1])
+            for h in range(2):
+                nc.scalar.activation(yn[t][:, h * HALF : (h + 1) * HALF], yg[t][:].indirect(half_of(n1_l, h)), COPY)
+
+        def make_z(t):
+            nc.vector.tensor_tensor(z_rows[:, t, :], yg[t][:], yn[t][:], ALU.subtract)
+
+        def quantise(woven, name):
+            words = new([P, S], U32, name + "_w")
+            scales = new([P, S], U8, name + "_s")
+            nc.vector.quantize_mx(out=words[:].bitcast(FP8X4), scales=scales[:], in_=woven[:])
+            return words, scales
+
+        fetch_d(0)
+        fetch_d(1)
+        cand_s = deal_columns(gather_packed(xs, U8, cand_l, "cand_s_raw"), U8, U8, "cand_s")
+        cand_w = deal_columns(gather_packed(xw, U32, cand_l, "cand_w_raw"), U32, I32, "cand_w")
+        put_ra(0)
+        fetch_y(0)
+        fetch_y(1)
+        ra1 = new([P, W], F32, "ra1")
+        nc.vector.scalar_tensor_tensor(ra1[:], old[1][:], 0.5, pa[1][:], ALU.mult, ALU.max)
+        nc.vector.tensor_copy(ds[1][:].indirect(n2_l[:, 0:12]), ra1[:, 0:192])
+        make_z(0)
+        make_z(1)
+        fetch_y(2)
+        fetch_y(3)
+        w3w = deal_fp4_words(w3w_raw, "w3w")
+        w3s = deal_columns(w3s_raw, U8, U8, "w3s")
+        make_z(2)
+        make_z(3)
+        fetch_d(2)
+        z_w, z_s = quantise(interleave(z_rows, S, "z_woven"), "z")
+        a_acc = [product("bank%d" % (PACK + t), w3w, w3s, t, z_w, z_s) for t in range(PACK)]
+        fetch_d(3)
+        nc.scalar.activation(ds[1][:].indirect(n2_l[:, 12:24]), ra1[:, 192:384], COPY)
+        put_ra(2)
+        put_ra(3)
+
+        a = [new([P, S], F32, "a%d" % t) for t in range(PACK)]
+        a4 = [new([P, S], F32, "a4_%d" % t) for t in range(PACK)]
+        for t in range(PACK):
+            nc.scalar.activation(a[t][:], a_acc[t][:], COPY)
+            for h in range(2):
+                nc.scalar.activation(a4[t][:, h * HALF : (h + 1) * HALF], a[t][:].indirect(half_of(n4_l, h)), COPY)
+
+        z2_rows = new([P, PACK, S], BF16, "z2_rows")
+        for t in range(PACK):
+            nc.vector.tensor_scalar(z2_rows[:, t, :], ds[t][:], gs_t[:, t : t + 1], None, ALU.mult)
+        z2_w, z2_s = quantise(interleave(z2_rows, S, "z2_woven"), "z2")
+        b_acc = [product("bank%d" % t, cand_w, cand_s, t, z2_w, z2_s) for t in range(PACK)]
+
+        scale = 0.75 * 0.0625
+        res = new([P, PACK, S], F32, "res")
+        woven = new([P, S * PACK], BF16, "res_woven")
+        out_words = new([P, S], U32, "out_words")
+        out_scales = new([P, S], U8, "out_scales")
+        out_rows = out_0.rearrange("(p t) j -> p t j", t=PACK)
+
+        for t in range(PACK):
+            b = new([P, S], F32, "b%d" % t)
+            b5 = new([P, S], F32, "b5_%d" % t)
+            first = new([P, S], F32, "first%d" % t)
+            second = new([P, S], F32, "second%d" % t)
+            nc.scalar.activation(b[:], b_acc[t][:], COPY, scale=scale)
+            nc.vector.tensor_tensor(second[:], a4[t][:], b[:], ALU.mult)
+            for h in range(2):
+                nc.scalar.activation(b5[:, h * HALF : (h + 1) * HALF], b[:].indirect(half_of(n5_l, h)), COPY)
+            pieces = [slice(0, S)] if t + 1 < PACK else [slice(0, HALF), slice(HALF, S)]
+            for cols in pieces:
+                nc.vector.tensor_tensor(first[:, cols], b5[:, cols], a[t][:, cols], ALU.mult)
+                nc.vector.tensor_tensor(res[:, t, cols], first[:, cols], second[:, cols], ALU.subtract)
+            nc.sync.dma_start(out_rows[:, t, :], res[:, t, :])
+        for h, copy in enumerate((nc.scalar.copy, nc.vector.tensor_copy)):
+            copy(
+                woven[:, h * HALF * PACK : (h + 1) * HALF * PACK].rearrange("p (c i t) -> p c t i", i=4, t=PACK),
+                res[:, :, h * HALF : (h + 1) * HALF].rearrange("p t (c i) -> p c t i", i=4),
+            )
+        nc.vector.quantize_mx(out=out_words[:].bitcast(FP8X4), scales=out_scales[:], in_=woven[:])
+        nc.sync.dma_start(out_1[0].rearrange("p n t -> p (n t)").bitcast(I32), out_words[:].bitcast(I32))
+        for q in range(4):
+            engine = nc.scalar if q % 2 == 0 else nc.sync
+            engine.dma_start(out_2[0, 4 * q : 4 * q + 4, :].bitcast(I32), out_scales[32 * q : 32 * q + 4, :].bitcast(I32))

@@ -5,7 +5,7 @@ import concourse.mybir as mybir
 K, T, S, W = 512, 2048, 512, 384
 P = 128
 PACK = 4
-HALF = S // 2
+HALVES = (slice(0, S // 2), slice(S // 2, S))
 FLOPS = 4 * 2 * 512 * 512 * 512
 
 F32 = mybir.dt.float32
@@ -42,9 +42,9 @@ def tile_picked_tfcdcrossbdifkmax_none_po_kernel(
             engine.memset(plane[:].bitcast(I32), 0)
             return plane
 
-        def load_scales(plane, src):
+        def load_scales(plane, src, queue):
             for q in range(4):
-                nc.sync.dma_start(plane[32 * q : 32 * q + 4, :].bitcast(I32), src[0, 4 * q : 4 * q + 4, :].bitcast(I32))
+                queue.dma_start(plane[32 * q : 32 * q + 4, :].bitcast(I32), src[0, 4 * q : 4 * q + 4, :].bitcast(I32))
 
         def load_fp4_words(src, name):
             raw = new([P, 2 * S], U8, name)
@@ -75,53 +75,57 @@ def tile_picked_tfcdcrossbdifkmax_none_po_kernel(
             nc.vector.tensor_copy(picked[:], table[:].indirect(lst[:]))
             return picked
 
-        def product(bank, lhs_words, lhs_scales, t, rhs_words, rhs_scales):
+        def product(acc, cols, lhs_words, lhs_scales, t, rhs_words, rhs_scales):
             per = lhs_words.shape[1] // PACK
             fmt = FP4X4 if per == 2 * P else FP8X4
-            acc = psum.tile([P, S], F32, name=bank)
             nc.tensor.matmul_mx(
-                out=acc[:],
+                out=acc[:, cols],
                 lhsT=lhs_words[:, per * t : per * (t + 1)].bitcast(fmt),
                 lhsT_scale=lhs_scales[:, P * t : P * (t + 1)],
-                rhs=rhs_words[:].bitcast(FP8X4),
-                rhs_scale=rhs_scales[:],
+                rhs=rhs_words[:, cols].bitcast(FP8X4),
+                rhs_scale=rhs_scales[:, cols],
                 start=True,
                 stop=True,
             )
+
+        def whole_product(bank, lhs_words, lhs_scales, t, rhs_words, rhs_scales):
+            acc = psum.tile([P, S], F32, name=bank)
+            product(acc, slice(0, S), lhs_words, lhs_scales, t, rhs_words, rhs_scales)
             return acc
 
-        def interleave(rows, width, name):
-            woven = new([P, width * PACK], BF16, name)
-            nc.vector.tensor_copy(
-                woven[:].rearrange("p (c i t) -> p c t i", i=4, t=PACK), rows[:].rearrange("p t (c i) -> p c t i", i=4)
+        def interleave(copy, woven, rows, cols):
+            copy(
+                woven[:, cols.start * PACK : cols.stop * PACK].rearrange("p (c i t) -> p c t i", i=4, t=PACK),
+                rows[:, :, cols].rearrange("p t (c i) -> p c t i", i=4),
             )
-            return woven
 
-        def half_of(lst, h):
-            return lst[:, h * HALF // 16 : (h + 1) * HALF // 16]
+        def entries(lst, cols):
+            return lst[:, cols.start // 16 : cols.stop // 16]
 
-        xs = zeroed_plane(T, "xs", nc.gpsimd)
-        w2s_raw = zeroed_plane(S, "w2s_raw", nc.vector)
-        w1s_raw = zeroed_plane(S, "w1s_raw", nc.vector)
-        w3s_raw = zeroed_plane(S, "w3s_raw", nc.vector)
-        load_scales(xs, x_scales)
+        w2s_raw = zeroed_plane(S, "w2s_raw", nc.gpsimd)
+        w1s_raw = zeroed_plane(S, "w1s_raw", nc.gpsimd)
+        w3s_raw = zeroed_plane(S, "w3s_raw", nc.gpsimd)
         two_l = load_list(two, "two_l")
+        xs = new([P, T], U8, "xs")
+        for q in range(4):
+            rows = x_scales[0, 4 * q : 4 * q + 4, :].bitcast(I32)
+            nc.sync.dma_start(xs[32 * q : 32 * q + 32, :].bitcast(I32), rows.unsqueeze(0).to_broadcast([8, 4, T // 4]))
         w2w_raw = load_fp4_words(w2_words, "w2w_raw")
         w1w_raw = load_fp4_words(w1_words, "w1w_raw")
         xw = new([P, T], U32, "xw")
         nc.sync.dma_start(xw[:].bitcast(I32), x_words[0].rearrange("p n t -> p (n t)").bitcast(I32))
-        load_scales(w2s_raw, w2_scales)
+        load_scales(w2s_raw, w2_scales, nc.sync)
         offs_l = load_list(offs, "offs_l")
         n3_l = load_list(n3, "n3_l")
         n2_l = load_list(n2, "n2_l")
-        load_scales(w1s_raw, w1_scales)
-        gn_t = load_gain(gn, "gn_t")
-        n1_l = load_list(n1, "n1_l")
+        load_scales(w1s_raw, w1_scales, nc.sync)
         cand_l = load_list(cand, "cand_l")
+        n1_l = load_list(n1, "n1_l")
+        gn_t = load_gain(gn, "gn_t")
         w3w_raw = load_fp4_words(w3_words, "w3w_raw")
-        load_scales(w3s_raw, w3_scales)
-        gs_t = load_gain(gs, "gs_t")
         n4_l = load_list(n4, "n4_l")
+        gs_t = load_gain(gs, "gs_t")
+        load_scales(w3s_raw, w3_scales, nc.sync)
         n5_l = load_list(n5, "n5_l")
 
         two_s = gather_packed(xs, U8, two_l, "two_s")
@@ -129,11 +133,11 @@ def tile_picked_tfcdcrossbdifkmax_none_po_kernel(
         w1w = deal_fp4_words(w1w_raw, "w1w")
         two_w = gather_packed(xw, U32, two_l, "two_w")
         w2s = deal_columns(w2s_raw, U8, U8, "w2s")
-        d_acc = [product("bank%d" % t, w2w, w2s, t, two_w, two_s) for t in range(PACK)]
+        d_acc = [whole_product("bank%d" % t, w2w, w2s, t, two_w, two_s) for t in range(2)]
         offs_s = gather_packed(xs, U8, offs_l, "offs_s")
-        offs_w = gather_packed(xw, U32, offs_l, "offs_w")
         w1s = deal_columns(w1s_raw, U8, U8, "w1s")
-        y_acc = [product("bank%d" % (PACK + t), w1w, w1s, t, offs_w, offs_s) for t in range(PACK)]
+        offs_w = gather_packed(xw, U32, offs_l, "offs_w")
+        y_acc = [whole_product("bank%d" % (PACK + t), w1w, w1s, t, offs_w, offs_s) for t in range(PACK)]
 
         ds = [new([P, S], F32, "ds%d" % t) for t in range(PACK)]
         pa = [new([P, W], F32, "pa%d" % t) for t in range(PACK)]
@@ -144,96 +148,176 @@ def tile_picked_tfcdcrossbdifkmax_none_po_kernel(
             nc.scalar.activation(pa[t][:], ds[t][:].indirect(n3_l[:]), COPY)
             nc.scalar.activation(old[t][:], ds[t][:].indirect(n2_l[:]), COPY)
 
-        def put_ra(t):
-            ra = new([P, W], F32, "ra")
-            nc.vector.scalar_tensor_tensor(ra[:], old[t][:], 0.5, pa[t][:], ALU.mult, ALU.max)
-            nc.vector.tensor_copy(ds[t][:].indirect(n2_l[:]), ra[:])
-
         yg = [new([P, S], F32, "yg%d" % t) for t in range(PACK)]
         yn = [new([P, S], F32, "yn%d" % t) for t in range(PACK)]
-        z_rows = new([P, PACK, S], BF16, "z_rows")
 
         def fetch_y(t):
             nc.scalar.activation(yg[t][:], y_acc[t][:], COPY, scale=gn_t[:, t : t + 1])
-            for h in range(2):
-                nc.scalar.activation(yn[t][:, h * HALF : (h + 1) * HALF], yg[t][:].indirect(half_of(n1_l, h)), COPY)
+            for cols in HALVES:
+                nc.scalar.activation(yn[t][:, cols], yg[t][:].indirect(entries(n1_l, cols)), COPY)
 
         def make_z(t):
             nc.vector.tensor_tensor(z_rows[:, t, :], yg[t][:], yn[t][:], ALU.subtract)
 
-        def quantise(woven, name):
-            words = new([P, S], U32, name + "_w")
-            scales = new([P, S], U8, name + "_s")
-            nc.vector.quantize_mx(out=words[:].bitcast(FP8X4), scales=scales[:], in_=woven[:])
-            return words, scales
+        def quantise(words, scales, woven, cols):
+            nc.vector.quantize_mx(
+                out=words[:, cols].bitcast(FP8X4), scales=scales[:, cols], in_=woven[:, cols.start * PACK : cols.stop * PACK]
+            )
+
+        def larger(t, name):
+            ra = new([P, W], F32, name)
+            nc.vector.scalar_tensor_tensor(ra[:], old[t][:], 0.5, pa[t][:], ALU.mult, ALU.max)
+            return ra
+
+        def put(t, ra):
+            nc.vector.tensor_copy(ds[t][:].indirect(n2_l[:]), ra[:])
+
+        def make_z2(t):
+            nc.vector.tensor_scalar(z2_rows[:, t, :], ds[t][:], gs_t[:, t : t + 1], None, ALU.mult)
 
         fetch_d(0)
         fetch_d(1)
-        cand_s = deal_columns(gather_packed(xs, U8, cand_l, "cand_s_raw"), U8, U8, "cand_s")
+        cand_s = deal_columns(gather_packed(xs, U8, cand_l, "w1s_raw"), U8, U8, "cand_s")
         cand_w = deal_columns(gather_packed(xw, U32, cand_l, "cand_w_raw"), U32, I32, "cand_w")
-        put_ra(0)
-        fetch_y(0)
-        fetch_y(1)
-        ra1 = new([P, W], F32, "ra1")
-        nc.vector.scalar_tensor_tensor(ra1[:], old[1][:], 0.5, pa[1][:], ALU.mult, ALU.max)
-        nc.vector.tensor_copy(ds[1][:].indirect(n2_l[:, 0:12]), ra1[:, 0:192])
-        make_z(0)
-        make_z(1)
-        fetch_y(2)
-        fetch_y(3)
+        ra0 = larger(0, "cand_w_raw")
+        ra1 = larger(1, "w1s_raw")
+        put(0, ra0)
+        put(1, ra1)
         w3w = deal_fp4_words(w3w_raw, "w3w")
         w3s = deal_columns(w3s_raw, U8, U8, "w3s")
-        make_z(2)
-        make_z(3)
+        z_rows = new([P, PACK, S], BF16, "z_rows")
+        for t in range(PACK):
+            fetch_y(t)
+            make_z(t)
+        d_acc.extend(whole_product("bank%d" % (PACK + t), w2w, w2s, t, two_w, two_s) for t in range(2, PACK))
         fetch_d(2)
-        z_w, z_s = quantise(interleave(z_rows, S, "z_woven"), "z")
-        a_acc = [product("bank%d" % (PACK + t), w3w, w3s, t, z_w, z_s) for t in range(PACK)]
+        z_woven = new([P, S * PACK], BF16, "z_woven")
+        z_w = new([P, S], U32, "z_w")
+        z_s = new([P, S], U8, "z_s")
+        interleave(nc.vector.tensor_copy, z_woven, z_rows, slice(0, S))
+        ra2 = larger(2, "z_rows")
+        quantise(z_w, z_s, z_woven, slice(0, S))
+        a_acc = [whole_product("bank%d" % t, w3w, w3s, t, z_w, z_s) for t in range(PACK)]
         fetch_d(3)
-        nc.scalar.activation(ds[1][:].indirect(n2_l[:, 12:24]), ra1[:, 192:384], COPY)
-        put_ra(2)
-        put_ra(3)
+        ra3 = larger(3, "ra3")
+        z2_rows = new([P, PACK, S], BF16, "z_woven")
+        make_z2(0)
+        make_z2(1)
+        put(3, ra3)
 
-        a = [new([P, S], F32, "a%d" % t) for t in range(PACK)]
+        a = [new([P, S], F32, "a%d" % t) for t in range(PACK - 1)]
         a4 = [new([P, S], F32, "a4_%d" % t) for t in range(PACK)]
-        for t in range(PACK):
-            nc.scalar.activation(a[t][:], a_acc[t][:], COPY)
-            for h in range(2):
-                nc.scalar.activation(a4[t][:, h * HALF : (h + 1) * HALF], a[t][:].indirect(half_of(n4_l, h)), COPY)
 
-        z2_rows = new([P, PACK, S], BF16, "z2_rows")
-        for t in range(PACK):
-            nc.vector.tensor_scalar(z2_rows[:, t, :], ds[t][:], gs_t[:, t : t + 1], None, ALU.mult)
-        z2_w, z2_s = quantise(interleave(z2_rows, S, "z2_woven"), "z2")
-        b_acc = [product("bank%d" % t, cand_w, cand_s, t, z2_w, z2_s) for t in range(PACK)]
+        def fetch_a(t, halves):
+            nc.scalar.activation(a[t][:], a_acc[t][:], COPY)
+            for cols in halves:
+                nc.scalar.activation(a4[t][:, cols], a[t][:].indirect(entries(n4_l, cols)), COPY)
+
+        share = slice(0, 384)
+        rest = slice(384, W)
+        nc.scalar.activation(ds[2][:].indirect(entries(n2_l, share)), ra2[:, share], COPY)
+        fetch_a(0, HALVES)
+
+        fetch_a(1, HALVES)
+        fetch_a(2, HALVES)
+
+        make_z2(3)
+        make_z2(2)
+        z2_woven = new([P, S * PACK], BF16, "z2_woven")
+        z2_w = new([P, S], U32, "z2_w")
+        z2_s = new([P, S], U8, "z2_s")
+        b_acc = [psum.tile([P, S], F32, name="bank%d" % (PACK + t)) for t in range(PACK)]
+        z2_parts = (slice(0, S),)
+        for cols in z2_parts:
+            interleave(nc.vector.tensor_copy, z2_woven, z2_rows, cols)
+        for cols in z2_parts:
+            quantise(z2_w, z2_s, z2_woven, cols)
+            for t in range(PACK):
+                product(b_acc[t], cols, cand_w, cand_s, t, z2_w, z2_s)
+        a.append(new([P, S], F32, "z2_woven"))
+        nc.vector.tensor_copy(a[3][:], a_acc[3][:])
+        for h, cols in enumerate(HALVES):
+            if h < 2:
+                nc.vector.tensor_copy(a4[3][:, cols], a[3][:].indirect(entries(n4_l, cols)))
+            else:
+                nc.scalar.activation(a4[3][:, cols], a[3][:].indirect(entries(n4_l, cols)), COPY)
 
         scale = 0.75 * 0.0625
-        res = new([P, PACK, S], F32, "res")
-        woven = new([P, S * PACK], BF16, "res_woven")
+        b = [new([P, S], F32, "b%d" % t) for t in range(PACK)]
+        b5 = [new([P, S], F32, "b5_%d" % t) for t in range(PACK)]
+        pieces = (slice(0, 256), slice(256, S))
+        early, late = 0, 1
+        width = [cols.stop - cols.start for cols in pieces]
+        first = [new([P, PACK, width[h]], F32, "first%d" % h) for h in range(2)]
+        second = new([P, PACK, S], F32, "second")
+        res = [new([P, PACK, width[h]], F32, "res%d" % h) for h in range(2)]
+        woven = [new([P, width[h] * PACK], BF16, "res_woven%d" % h) for h in range(2)]
         out_words = new([P, S], U32, "out_words")
         out_scales = new([P, S], U8, "out_scales")
         out_rows = out_0.rearrange("(p t) j -> p t j", t=PACK)
+        out_cols = out_1[0].rearrange("p n t -> p (n t)").bitcast(I32)
 
-        for t in range(PACK):
-            b = new([P, S], F32, "b%d" % t)
-            b5 = new([P, S], F32, "b5_%d" % t)
-            first = new([P, S], F32, "first%d" % t)
-            second = new([P, S], F32, "second%d" % t)
-            nc.scalar.activation(b[:], b_acc[t][:], COPY, scale=scale)
-            nc.vector.tensor_tensor(second[:], a4[t][:], b[:], ALU.mult)
-            for h in range(2):
-                nc.scalar.activation(b5[:, h * HALF : (h + 1) * HALF], b[:].indirect(half_of(n5_l, h)), COPY)
-            pieces = [slice(0, S)] if t + 1 < PACK else [slice(0, HALF), slice(HALF, S)]
-            for cols in pieces:
-                nc.vector.tensor_tensor(first[:, cols], b5[:, cols], a[t][:, cols], ALU.mult)
-                nc.vector.tensor_tensor(res[:, t, cols], first[:, cols], second[:, cols], ALU.subtract)
-            nc.sync.dma_start(out_rows[:, t, :], res[:, t, :])
-        for h, copy in enumerate((nc.scalar.copy, nc.vector.tensor_copy)):
-            copy(
-                woven[:, h * HALF * PACK : (h + 1) * HALF * PACK].rearrange("p (c i t) -> p c t i", i=4, t=PACK),
-                res[:, :, h * HALF : (h + 1) * HALF].rearrange("p t (c i) -> p c t i", i=4),
-            )
-        nc.vector.quantize_mx(out=out_words[:].bitcast(FP8X4), scales=out_scales[:], in_=woven[:])
-        nc.sync.dma_start(out_1[0].rearrange("p n t -> p (n t)").bitcast(I32), out_words[:].bitcast(I32))
+        def leave_bank(t):
+            if t in (1,):
+                nc.vector.tensor_scalar(b[t][:], b_acc[t][:], scale, None, ALU.mult)
+            else:
+                nc.scalar.activation(b[t][:], b_acc[t][:], COPY, scale=scale)
+
+        def fetch_b(t, h):
+            nc.scalar.activation(b5[t][:, pieces[h]], b[t][:].indirect(entries(n5_l, pieces[h])), COPY)
+
+        def second_from_bank(t):
+            nc.vector.scalar_tensor_tensor(second[:, t, :], b_acc[t][:], scale, a4[t][:], ALU.mult, ALU.mult)
+
+        def second_from_copy(t):
+            nc.vector.tensor_tensor(second[:, t, :], a4[t][:], b[t][:], ALU.mult)
+
+        def make_first(t, h):
+            nc.vector.tensor_tensor(first[h][:, t, :], b5[t][:, pieces[h]], a[t][:, pieces[h]], ALU.mult)
+
+        def make_res(tiles, h):
+            nc.vector.tensor_tensor(res[h][:, tiles, :], first[h][:, tiles, :], second[:, tiles, pieces[h]], ALU.subtract)
+
+        def hand_on(h):
+            cols = pieces[h]
+            nc.vector.quantize_mx(out=out_words[:, cols].bitcast(FP8X4), scales=out_scales[:, cols], in_=woven[h][:])
+            nc.sync.dma_start(out_cols[:, cols], out_words[:, cols].bitcast(I32))
+
+        leave_bank(0)
+        leave_bank(1)
+        fetch_b(0, early)
+        leave_bank(2)
+        second_from_copy(0)
+        make_first(0, early)
+        fetch_b(1, early)
+        leave_bank(3)
+        second_from_copy(1)
+        make_res(slice(0, 1), early)
+        make_first(1, early)
+        fetch_b(2, early)
+        second_from_copy(2)
+        make_res(slice(1, 2), early)
+        make_first(2, early)
+        fetch_b(3, early)
+        second_from_copy(3)
+        make_res(slice(2, 3), early)
+        make_first(3, early)
+        fetch_b(0, late)
+        fetch_b(1, late)
+        fetch_b(2, late)
+        fetch_b(3, late)
+        make_first(0, late)
+        make_res(slice(3, 4), early)
+        nc.sync.dma_start(out_rows[:, :, pieces[early]], res[early][:])
+        interleave(nc.scalar.copy, woven[early], res[early], slice(0, 256))
+        make_first(1, late)
+        make_first(2, late)
+        make_first(3, late)
+        make_res(slice(0, 4), late)
+        nc.sync.dma_start(out_rows[:, :, pieces[late]], res[late][:])
+        interleave(nc.vector.tensor_copy, woven[late], res[late], slice(0, 256))
+        hand_on(early)
+        hand_on(late)
         for q in range(4):
             engine = nc.scalar if q % 2 == 0 else nc.sync
             engine.dma_start(out_2[0, 4 * q : 4 * q + 4, :].bitcast(I32), out_scales[32 * q : 32 * q + 4, :].bitcast(I32))

from contextlib import ExitStack

import concourse.mybir as mybir

K, T, S, W = 512, 2048, 512, 384
P = 128
PACK = 4
HALVES = (slice(0, S // 2), slice(S // 2, S))
FLOPS = 4 * 2 * 512 * 512 * 512

F32 = mybir.dt.float32
BF16 = mybir.dt.bfloat16
I32 = mybir.dt.int32
U32 = mybir.dt.uint32
U16 = mybir.dt.uint16
U8 = mybir.dt.uint8
FP8X4 = mybir.dt.float8_e4m3fn_x4
FP4X4 = mybir.dt.float4_e2m1fn_x4
ALU = mybir.AluOpType
COPY = mybir.ActivationFunctionType.Copy


def tile_picked_tfcdcrossbdifkmax_none_po_kernel(
    tc, x_words, x_scales, w1_words, w1_scales, w2_words, w2_scales, gn, w3_words, w3_scales, gs,
    offs, two, n1, n2, n3, cand, n4, n5, out_0, out_1, out_2,
):
    nc = tc.nc
    with ExitStack() as ctx:
        sb = ctx.enter_context(tc.tile_pool(name="sb", bufs=1))
        psum = ctx.enter_context(tc.psum_pool(name="psum", bufs=1))

        def new(shape, dtype, name):
            return sb.tile(shape, dtype, name=name, align_bytes=64)

        def load_list(src, name):
            lst = new(list(src.shape), U16, name)
            nc.sync.dma_start(lst[:], src)
            return lst

        def zeroed_plane(width, name, engine):
            plane = new([P, width], U8, name)
            engine.memset(plane[:].bitcast(I32), 0)
            return plane

        def load_scales(plane, src, queue):
            for q in range(4):
                queue.dma_start(plane[32 * q : 32 * q + 4, :].bitcast(I32), src[0, 4 * q : 4 * q + 4, :].bitcast(I32))

        def load_fp4_words(src, name):
            raw = new([P, 2 * S], U8, name)
            nc.sync.dma_start(raw[:].bitcast(I32), src[0].bitcast(I32))
            return raw

        def load_gain(src, name):
            gain = new([P, PACK], F32, name)
            nc.sync.dma_start(gain[:], src.rearrange("(p t) o -> p (t o)", t=PACK))
            return gain

        def deal_fp4_words(raw, name):
            dealt = new([P, 2 * S], U8, name)
            nc.vector.tensor_copy(
                dealt[:].rearrange("p (t m b) -> p t m b", t=PACK, b=2), raw[:].rearrange("p (m t b) -> p t m b", t=PACK, b=2)
            )
            return dealt

        def deal_columns(raw, dtype, view, name):
            dealt = new([P, S], dtype, name)
            nc.vector.tensor_copy(
                dealt[:].bitcast(view).rearrange("p (t m) -> p t m", t=PACK), raw[:].bitcast(view).rearrange("p (m t) -> p t m", t=PACK)
            )
            return dealt

        def gather_packed(table, dtype, lst, name):
            picked = new([P, S], dtype, name)
            nc.vector.tensor_copy(picked[:], table[:].indirect(lst[:]))
            return picked

        def product(acc, cols, lhs_words, lhs_scales, t, rhs_words, rhs_scales):
            per = lhs_words.shape[1] // PACK
            fmt = FP4X4 if per == 2 * P else FP8X4
            nc.tensor.matmul_mx(
                out=acc[:, cols],
                lhsT=lhs_words[:, per * t : per * (t + 1)].bitcast(fmt),
                lhsT_scale=lhs_scales[:, P * t : P * (t + 1)],
                rhs=rhs_words[:, cols].bitcast(FP8X4),
                rhs_scale=rhs_scales[:, cols],
                start=True,
                stop=True,
            )

        def whole_product(bank, lhs_words, lhs_scales, t, rhs_words, rhs_scales):
            acc = psum.tile([P, S], F32, name=bank)
            product(acc, slice(0, S), lhs_words, lhs_scales, t, rhs_words, rhs_scales)
            return acc

        def interleave(copy, woven, rows, cols):
            copy(
                woven[:, cols.start * PACK : cols.stop * PACK].rearrange("p (c i t) -> p c t i", i=4, t=PACK),
                rows[:, :, cols].rearrange("p t (c i) -> p c t i", i=4),
            )

        def entries(lst, cols):
            return lst[:, cols.start // 16 : cols.stop // 16]

        w2s_raw = zeroed_plane(S, "w2s_raw", nc.gpsimd)
        w1s_raw = zeroed_plane(S, "w1s_raw", nc.gpsimd)
        w3s_raw = zeroed_plane(S, "w3s_raw", nc.gpsimd)
        two_l = load_list(two, "two_l")
        xs = new([P, T], U8, "xs")
        for q in range(4):
            rows = x_scales[0, 4 * q : 4 * q + 4, :].bitcast(I32)
            nc.sync.dma_start(xs[32 * q : 32 * q + 32, :].bitcast(I32), rows.unsqueeze(0).to_broadcast([8, 4, T // 4]))
        w2w_raw = load_fp4_words(w2_words, "w2w_raw")
        w1w_raw = load_fp4_words(w1_words, "w1w_raw")
        xw = new([P, T], U32, "xw")
        nc.sync.dma_start(xw[:].bitcast(I32), x_words[0].rearrange("p n t -> p (n t)").bitcast(I32))
        load_scales(w2s_raw, w2_scales, nc.sync)
        offs_l = load_list(offs, "offs_l")
        n3_l = load_list(n3, "n3_l")
        n2_l = load_list(n2, "n2_l")
        load_scales(w1s_raw, w1_scales, nc.sync)
        cand_l = load_list(cand, "cand_l")
        n1_l = load_list(n1, "n1_l")
        gn_t = load_gain(gn, "gn_t")
        w3w_raw = load_fp4_words(w3_words, "w3w_raw")
        n4_l = load_list(n4, "n4_l")
        gs_t = load_gain(gs, "gs_t")
        load_scales(w3s_raw, w3_scales, nc.sync)
        n5_l = load_list(n5, "n5_l")

        two_s = gather_packed(xs, U8, two_l, "two_s")
        w2w = deal_fp4_words(w2w_raw, "w2w")
        w1w = deal_fp4_words(w1w_raw, "w1w")
        two_w = gather_packed(xw, U32, two_l, "two_w")
        w2s = deal_columns(w2s_raw, U8, U8, "w2s")
        d_acc = [whole_product("bank%d" % t, w2w, w2s, t, two_w, two_s) for t in range(2)]
        offs_s = gather_packed(xs, U8, offs_l, "offs_s")
        w1s = deal_columns(w1s_raw, U8, U8, "w1s")
        offs_w = gather_packed(xw, U32, offs_l, "offs_w")
        y_acc = [whole_product("bank%d" % (PACK + t), w1w, w1s, t, offs_w, offs_s) for t in range(PACK)]

        ds = [new([P, S], F32, "ds%d" % t) for t in range(PACK)]
        pa = [new([P, W], F32, "pa%d" % t) for t in range(PACK)]
        old = [new([P, W], F32, "old%d" % t) for t in range(PACK)]

        def fetch_d(t):
            nc.scalar.activation(ds[t][:], d_acc[t][:], COPY)
            nc.scalar.activation(pa[t][:], ds[t][:].indirect(n3_l[:]), COPY)
            nc.scalar.activation(old[t][:], ds[t][:].indirect(n2_l[:]), COPY)

        yg = [new([P, S], F32, "yg%d" % t) for t in range(PACK)]
        yn = [new([P, S], F32, "yn%d" % t) for t in range(PACK)]

        def fetch_y(t):
            nc.scalar.activation(yg[t][:], y_acc[t][:], COPY, scale=gn_t[:, t : t + 1])
            for cols in HALVES:
                nc.scalar.activation(yn[t][:, cols], yg[t][:].indirect(entries(n1_l, cols)), COPY)

        def make_z(t):
            nc.vector.tensor_tensor(z_rows[:, t, :], yg[t][:], yn[t][:], ALU.subtract)

        def quantise(words, scales, woven, cols):
            nc.vector.quantize_mx(
                out=words[:, cols].bitcast(FP8X4), scales=scales[:, cols], in_=woven[:, cols.start * PACK : cols.stop * PACK]
            )

        def larger(t, name):
            ra = new([P, W], F32, name)
            nc.vector.scalar_tensor_tensor(ra[:], old[t][:], 0.5, pa[t][:], ALU.mult, ALU.max)
            return ra

        def put(t, ra):
            nc.vector.tensor_copy(ds[t][:].indirect(n2_l[:]), ra[:])

        def make_z2(t):
            nc.vector.tensor_scalar(z2_rows[:, t, :], ds[t][:], gs_t[:, t : t + 1], None, ALU.mult)

        fetch_d(0)
        fetch_d(1)
        cand_s = deal_columns(gather_packed(xs, U8, cand_l, "w1s_raw"), U8, U8, "cand_s")
        cand_w = deal_columns(gather_packed(xw, U32, cand_l, "cand_w_raw"), U32, I32, "cand_w")
        ra0 = larger(0, "cand_w_raw")
        ra1 = larger(1, "w1s_raw")
        put(0, ra0)
        put(1, ra1)
        w3w = deal_fp4_words(w3w_raw, "w3w")
        w3s = deal_columns(w3s_raw, U8, U8, "w3s")
        z_rows = new([P, PACK, S], BF16, "z_rows")
        for t in range(PACK):
            fetch_y(t)
            make_z(t)
        d_acc.extend(whole_product("bank%d" % (PACK + t), w2w, w2s, t, two_w, two_s) for t in range(2, PACK))
        fetch_d(2)
        z_woven = new([P, S * PACK], BF16, "z_woven")
        z_w = new([P, S], U32, "z_w")
        z_s = new([P, S], U8, "z_s")
        interleave(nc.vector.tensor_copy, z_woven, z_rows, slice(0, S))
        ra2 = larger(2, "z_rows")
        quantise(z_w, z_s, z_woven, slice(0, S))
        a_acc = [whole_product("bank%d" % t, w3w, w3s, t, z_w, z_s) for t in range(PACK)]
        fetch_d(3)
        ra3 = larger(3, "ra3")
        z2_rows = new([P, PACK, S], BF16, "z_woven")
        make_z2(0)
        make_z2(1)
        put(3, ra3)

        a = [new([P, S], F32, "a%d" % t) for t in range(PACK - 1)]
        a4 = [new([P, S], F32, "a4_%d" % t) for t in range(PACK)]

        def fetch_a(t, halves):
            nc.scalar.activation(a[t][:], a_acc[t][:], COPY)
            for cols in halves:
                nc.scalar.activation(a4[t][:, cols], a[t][:].indirect(entries(n4_l, cols)), COPY)

        share = slice(0, 384)
        rest = slice(384, W)
        nc.scalar.activation(ds[2][:].indirect(entries(n2_l, share)), ra2[:, share], COPY)
        fetch_a(0, HALVES)

        fetch_a(1, HALVES)
        fetch_a(2, HALVES)

        make_z2(3)
        make_z2(2)
        z2_woven = new([P, S * PACK], BF16, "z2_woven")
        z2_w = new([P, S], U32, "z2_w")
        z2_s = new([P, S], U8, "z2_s")
        b_acc = [psum.tile([P, S], F32, name="bank%d" % (PACK + t)) for t in range(PACK)]
        z2_parts = (slice(0, S),)
        for cols in z2_parts:
            interleave(nc.vector.tensor_copy, z2_woven, z2_rows, cols)
        for cols in z2_parts:
            quantise(z2_w, z2_s, z2_woven, cols)
            for t in range(PACK):
                product(b_acc[t], cols, cand_w, cand_s, t, z2_w, z2_s)
        a.append(new([P, S], F32, "z2_woven"))
        nc.vector.tensor_copy(a[3][:], a_acc[3][:])
        for h, cols in enumerate(HALVES):
            if h < 2:
                nc.vector.tensor_copy(a4[3][:, cols], a[3][:].indirect(entries(n4_l, cols)))
            else:
                nc.scalar.activation(a4[3][:, cols], a[3][:].indirect(entries(n4_l, cols)), COPY)

        scale = 0.75 * 0.0625
        b = [new([P, S], F32, "b%d" % t) for t in range(PACK)]
        b5 = [new([P, S], F32, "b5_%d" % t) for t in range(PACK)]
        pieces = (slice(0, 256), slice(256, S))
        early, late = 0, 1
        width = [cols.stop - cols.start for cols in pieces]
        first = [new([P, PACK, width[h]], F32, "first%d" % h) for h in range(2)]
        second = new([P, PACK, S], F32, "second")
        res = [new([P, PACK, width[h]], F32, "res%d" % h) for h in range(2)]
        woven = [new([P, width[h] * PACK], BF16, "res_woven%d" % h) for h in range(2)]
        out_words = new([P, S], U32, "out_words")
        out_scales = new([P, S], U8, "out_scales")
        out_rows = out_0.rearrange("(p t) j -> p t j", t=PACK)
        out_cols = out_1[0].rearrange("p n t -> p (n t)").bitcast(I32)

        def leave_bank(t):
            if t in (1,):
                nc.vector.tensor_scalar(b[t][:], b_acc[t][:], scale, None, ALU.mult)
            else:
                nc.scalar.activation(b[t][:], b_acc[t][:], COPY, scale=scale)

        def fetch_b(t, h):
            nc.scalar.activation(b5[t][:, pieces[h]], b[t][:].indirect(entries(n5_l, pieces[h])), COPY)

        def second_from_bank(t):
            nc.vector.scalar_tensor_tensor(second[:, t, :], b_acc[t][:], scale, a4[t][:], ALU.mult, ALU.mult)

        def second_from_copy(t):
            nc.vector.tensor_tensor(second[:, t, :], a4[t][:], b[t][:], ALU.mult)

        def make_first(t, h):
            nc.vector.tensor_tensor(first[h][:, t, :], b5[t][:, pieces[h]], a[t][:, pieces[h]], ALU.mult)

        def make_res(tiles, h):
            nc.vector.tensor_tensor(res[h][:, tiles, :], first[h][:, tiles, :], second[:, tiles, pieces[h]], ALU.subtract)

        def hand_on(h):
            cols = pieces[h]
            nc.vector.quantize_mx(out=out_words[:, cols].bitcast(FP8X4), scales=out_scales[:, cols], in_=woven[h][:])
            nc.sync.dma_start(out_cols[:, cols], out_words[:, cols].bitcast(I32))

        leave_bank(0)
        leave_bank(1)
        fetch_b(0, early)
        leave_bank(2)
        second_from_copy(0)
        make_first(0, early)
        fetch_b(1, early)
        leave_bank(3)
        second_from_copy(1)
        make_res(slice(0, 1), early)
        make_first(1, early)
        fetch_b(2, early)
        second_from_copy(2)
        make_res(slice(1, 2), early)
        make_first(2, early)
        fetch_b(3, early)
        second_from_copy(3)
        make_res(slice(2, 3), early)
        make_first(3, early)
        fetch_b(0, late)
        fetch_b(1, late)
        fetch_b(2, late)
        fetch_b(3, late)
        make_first(0, late)
        make_res(slice(3, 4), early)
        nc.sync.dma_start(out_rows[:, :, pieces[early]], res[early][:])
        interleave(nc.scalar.copy, woven[early], res[early], slice(0, 256))
        make_first(1, late)
        make_first(2, late)
        make_first(3, late)
        make_res(slice(0, 4), late)
        nc.sync.dma_start(out_rows[:, :, pieces[late]], res[late][:])
        interleave(nc.vector.tensor_copy, woven[late], res[late], slice(0, 256))
        hand_on(early)
        hand_on(late)
        for q in range(4):
            engine = nc.scalar if q % 2 == 0 else nc.sync
            engine.dma_start(out_2[0, 4 * q : 4 * q + 4, :].bitcast(I32), out_scales[32 * q : 32 * q + 4, :].bitcast(I32))
